import numpy as np
import ml_dtypes


def mxq(x, axis, fmt="e4m3"):
    dtype, down = {"e4m3": (ml_dtypes.float8_e4m3fn, 7), "e5m2": (ml_dtypes.float8_e5m2, 14)}[fmt]
    v = np.moveaxis(np.asarray(x, np.float32).astype(ml_dtypes.bfloat16).astype(np.float64), axis, -1)
    blocks = v.reshape(v.shape[:-1] + (-1, 32))
    amax = np.abs(blocks).max(-1, keepdims=True)
    byte = np.maximum(np.where(amax > 0, np.frexp(amax)[1] - 1 + 127, 0) - down, 1)
    scale = np.exp2(byte - 127.0)
    codes = (blocks / scale).astype(np.float32).astype(dtype).astype(np.float64)
    return np.moveaxis((codes * scale).reshape(v.shape), -1, axis)


WIDE = False


def mx_kscale(k):
    if not WIDE:
        return np.ones(k)
    levels = np.array([10, -10, 5, -5, 0])
    if k % 512:
        return np.exp2(np.random.permutation(np.resize(levels, k // 32))).repeat(32)
    a = np.empty((k // 512, 16))
    for p in range(k // 512):
        a[p, :8] = np.random.permutation(np.resize(levels, 8))
        for g in range(8):
            far = levels[np.abs(levels - a[p, g]) >= 10]
            a[p, g + 8] = far[np.random.randint(len(far))]
    return np.exp2(a.ravel()).repeat(32)


def f64(x):
    return np.asarray(x).astype(np.float64)


def striped(idx):
    return np.tile(idx.reshape(-1, 16).T, (8, 1)).astype(np.uint16)


def unstriped(offs):
    return offs[:16].T.reshape(-1).astype(np.int64)


def silu(v):
    return v / (1.0 + np.exp(-np.maximum(v, -700.0)))


K, T, E, C, H, N = 1024, 1024, 8, 128, 512, 256


def by_expert(wq, xq):
    return np.concatenate([wq[e].T @ xq[:, e * C:(e + 1) * C] for e in range(E)], axis=1)


def setup_inputs():
    n = np.random.standard_normal
    s = mx_kscale(K)[:, None]
    u = mx_kscale(H)
    return {
        "xT": (n((K, T)) * s).astype(np.float32),
        "w1": (n((E, K, H)) / np.sqrt(K) / s[None]).astype(np.float32),
        "w3": (n((E, K, H)) / np.sqrt(K) / s[None] * u[None, None, :]).astype(np.float32),
        "w2": (n((E, H, N)) / np.sqrt(H) / u[None, :, None]).astype(np.float32),
        "gate": np.tile(np.random.uniform(0.2, 1.0, E * C), (N, 1)).astype(np.float32),
        "offs": striped(np.random.permutation(T)[:E * C]),
    }


def reference(xT, w1, w3, w2, gate, offs):
    idx = unstriped(offs)
    xq = mxq(f64(xT)[:, idx], 0, "e4m3")
    h = silu(by_expert(mxq(f64(w1), 1, "e4m3"), xq))
    h = h * by_expert(mxq(f64(w3), 1, "e4m3"), xq)
    y = by_expert(mxq(f64(w2), 1, "e4m3"), mxq(h, 0, "e4m3"))
    out = np.zeros((N, T))
    out[:, idx] = f64(gate) * y
    return out

@@ -1,0 +1,266 @@
+from contextlib import ExitStack
+
+import concourse.mybir as mybir
+
+K, T, E, C, H, N = 1024, 1024, 8, 128, 512, 256
+FLOPS = 2 * E * C * (2 * K * H + H * N)
+
+F32 = mybir.dt.float32
+BF16 = mybir.dt.bfloat16
+U32 = mybir.dt.uint32
+U16 = mybir.dt.uint16
+U8 = mybir.dt.uint8
+FP8X4 = mybir.dt.float8_e4m3fn_x4
+MULT = mybir.AluOpType.mult
+SILU = mybir.ActivationFunctionType.Silu
+
+P = 128
+PACK = 4
+PASSES = K // (P * PACK)
+SLOTS = E * C
+BLOCKS = N // P
+LINE = 4
+
+STAGE_BUFS = 11
+LOADS_BEFORE_GATE = 2 * PASSES + 2 * PASSES + 1
+GATHER = 512
+LATE = 2
+SCALAR_TAKES_BOTH = (0, 2, 4)
+VECTOR_GROUPS_W3 = 84
+VECTOR_GROUPS_W2 = 40
+
+
+def tile_routed_moe_kernel(tc, xT, w1, w3, w2, gate, offs, out):
+    nc = tc.nc
+    with ExitStack() as ctx:
+        keep = ctx.enter_context(tc.tile_pool(name="keep", bufs=1))
+        stage = ctx.enter_context(tc.tile_pool(name="stage", bufs=STAGE_BUFS))
+        grouped_pool = ctx.enter_context(tc.tile_pool(name="grouped", bufs=3))
+        first_codes = ctx.enter_context(tc.tile_pool(name="first_codes", bufs=5))
+        second_codes = ctx.enter_context(tc.tile_pool(name="second_codes", bufs=3))
+        small = ctx.enter_context(tc.tile_pool(name="small", bufs=3))
+        psum = ctx.enter_context(tc.psum_pool(name="psum", bufs=2))
+
+        offs_t = keep.tile([P, SLOTS // 16], U16, name="offs_t")
+        nc.sync.dma_start(offs_t[:], offs)
+
+        table_in = keep.tile([P, 1], F32, name="table_in")
+        table_out = keep.tile([P, 1], F32, name="table_out")
+        nc.vector.memset(table_in[:], 0.0)
+        nc.scalar.activation(out=table_out[:], in_=table_in[:], func=SILU)
+
+        x_view = xT.rearrange("(g p u r) n -> g u p r n", g=PASSES, p=P, u=2, r=2)
+        first_views = (
+            w1.rearrange("e (g p j) c -> e g p j c", g=PASSES, p=P, j=PACK),
+            w3.rearrange("e (g p j) c -> e g p j c", g=PASSES, p=P, j=PACK),
+        )
+        w2_view = w2.rearrange("e (p j) n -> e p j n", p=P, j=PACK)
+
+        loads = []
+        for g in range(PASSES):
+            for u in range(2):
+                loads.append(("x", g, u))
+        for e in range(E):
+            for m in range(2):
+                for g in range(PASSES):
+                    loads.append(("first", e, m, g))
+            if e < E - LATE:
+                loads.append(("second", e))
+        for e in range(E - LATE, E):
+            loads.append(("second", e))
+        staged = {}
+        started = {"count": 0}
+
+        def start_next_load():
+            if started["count"] < len(loads):
+                key = loads[started["count"]]
+                if key[0] == "x":
+                    raw = stage.tile([P, 2, T], F32, name="raw", tag="raw")
+                    nc.sync.dma_start(raw[:], x_view[key[1], key[2], :, :, :])
+                elif key[0] == "first":
+                    raw = stage.tile([P, PACK, H], F32, name="raw", tag="raw")
+                    nc.sync.dma_start(raw[:], first_views[key[2]][key[1], key[3], :, :, :])
+                else:
+                    raw = stage.tile([P, PACK, N], F32, name="raw", tag="raw")
+                    nc.sync.dma_start(raw[:], w2_view[key[1], :, :, :])
+                staged[key] = raw
+            started["count"] = started["count"] + 1
+
+        gate_sb = []
+        window = []
+        for i in range(LOADS_BEFORE_GATE):
+            start_next_load()
+        for b in range(BLOCKS):
+            gate_b = keep.tile([P, SLOTS], F32, name="gate%d" % b)
+            nc.sync.dma_start(gate_b[:], gate[b * P : (b + 1) * P, :])
+            gate_sb.append(gate_b)
+            window_b = keep.tile([P, T], F32, name="window%d" % b)
+            window.append(window_b)
+        for i in range(LOADS_BEFORE_GATE, STAGE_BUFS):
+            start_next_load()
+
+        x_codes = []
+        x_scales = []
+        for g in range(PASSES):
+            x_grouped = keep.tile([P, PACK * SLOTS], BF16, name="x_grouped%d" % g, align_bytes=64)
+            x_words = x_grouped[:].bitcast(U32).rearrange("p (s u) -> p s u", u=2)
+            for u in range(2):
+                raw = staged[("x", g, u)]
+                x_pairs = keep.tile([P, 2 * T], BF16, name="x_pairs%d%d" % (g, u))
+                nc.scalar.copy(
+                    out=x_pairs[:].rearrange("p (c i r) -> p c r i", i=LINE, r=2),
+                    in_=raw[:].rearrange("p r (c i) -> p c r i", i=LINE),
+                )
+                start_next_load()
+                for s0 in range(0, SLOTS, GATHER):
+                    nc.vector.tensor_copy(
+                        out=x_words[:, s0 : s0 + GATHER, u],
+                        in_=x_pairs[:].bitcast(U32).indirect(offs_t[:, s0 // 16 : (s0 + GATHER) // 16]),
+                    )
+            x_codes_g = keep.tile([P, SLOTS], U32, name="x_codes%d" % g, align_bytes=64)
+            x_scales_g = keep.tile([P, SLOTS], U8, name="x_scales%d" % g, align_bytes=64)
+            nc.vector.quantize_mx(out=x_codes_g[:].bitcast(FP8X4), scales=x_scales_g[:], in_=x_grouped[:])
+            x_codes.append(x_codes_g)
+            x_scales.append(x_scales_g)
+
+        def first_layer(e):
+            slots = slice(e * C, (e + 1) * C)
+            last = e == E - 1
+            quantised = []
+            for m in range(2):
+                w_grouped = grouped_pool.tile([P, PASSES * PACK * H], BF16, name="w_grouped", tag="w_grouped", align_bytes=64)
+                codes = first_codes.tile([P, PASSES * H], U32, name="w_codes", tag="w_codes", align_bytes=64)
+                scales = first_codes.tile([P, PASSES * H], U8, name="w_scales", tag="w_scales", align_bytes=64)
+                for g in range(PASSES):
+                    raw = staged[("first", e, m, g)]
+                    dst = w_grouped[:, g * PACK * H : (g + 1) * PACK * H].rearrange("p (t q j) -> p q j t", t=PACK, q=P, j=PACK)
+                    src = raw[:].rearrange("p j (q t) -> p q j t", t=PACK)
+                    if last and m == 1:
+                        nc.vector.tensor_copy(out=dst[:, :VECTOR_GROUPS_W3, :, :], in_=src[:, :VECTOR_GROUPS_W3, :, :])
+                        nc.scalar.copy(out=dst[:, VECTOR_GROUPS_W3:, :, :], in_=src[:, VECTOR_GROUPS_W3:, :, :])
+                    elif g == 0 or (m == 0 and e in SCALAR_TAKES_BOTH):
+                        nc.scalar.copy(out=dst, in_=src)
+                    else:
+                        nc.vector.tensor_copy(out=dst, in_=src)
+                    start_next_load()
+                    if last:
+                        calls = 2 if m == 1 and g == PASSES - 1 else 1
+                        width = H // calls
+                        for c0 in range(g * H, (g + 1) * H, width):
+                            nc.vector.quantize_mx(
+                                out=codes[:, c0 : c0 + width].bitcast(FP8X4),
+                                scales=scales[:, c0 : c0 + width],
+                                in_=w_grouped[:, PACK * c0 : PACK * (c0 + width)],
+                            )
+                if not last:
+                    nc.vector.quantize_mx(out=codes[:].bitcast(FP8X4), scales=scales[:], in_=w_grouped[:])
+                quantised.append((codes, scales))
+
+            a_ps = psum.tile([P, PACK, C], F32, name="a_ps", tag="a_ps")
+            b_ps = psum.tile([P, PACK, C], F32, name="b_ps", tag="b_ps")
+            for m, acc in ((0, a_ps), (1, b_ps)):
+                codes, scales = quantised[m]
+                for t in range(PACK):
+                    for g in range(PASSES):
+                        cols = slice(g * H + t * P, g * H + (t + 1) * P)
+                        nc.tensor.matmul_mx(
+                            out=acc[:, t, :],
+                            lhsT=codes[:, cols].bitcast(FP8X4),
+                            lhsT_scale=scales[:, cols],
+                            rhs=x_codes[g][:, slots].bitcast(FP8X4),
+                            rhs_scale=x_scales[g][:, slots],
+                            start=(g == 0),
+                            stop=(g == PASSES - 1),
+                        )
+            silu_a = small.tile([P, C, PACK], F32, name="silu_a", tag="silu_a")
+            nc.scalar.activation(out=silu_a[:], in_=a_ps[:].rearrange("p t c -> p c t"), func=SILU)
+            h_grouped = small.tile([P, C, PACK], BF16, name="h_grouped", tag="h_grouped", align_bytes=64)
+            nc.vector.tensor_tensor(out=h_grouped[:], in0=b_ps[:].rearrange("p t c -> p c t"), in1=silu_a[:], op=MULT)
+            h_codes = small.tile([P, C], U32, name="h_codes", tag="h_codes", align_bytes=64)
+            h_scales = small.tile([P, C], U8, name="h_scales", tag="h_scales", align_bytes=64)
+            nc.vector.quantize_mx(
+                out=h_codes[:].bitcast(FP8X4), scales=h_scales[:], in_=h_grouped[:].rearrange("p c t -> p (c t)")
+            )
+            return h_codes, h_scales
+
+        def second_weights(e):
+            raw = staged[("second", e)]
+            v_grouped = grouped_pool.tile([P, PACK * N], BF16, name="v_grouped", tag="v_grouped", align_bytes=64)
+            dst = v_grouped[:].rearrange("p (c i j) -> p c j i", i=LINE, j=PACK)
+            src = raw[:].rearrange("p j (c i) -> p c j i", i=LINE)
+            if e == E - 1:
+                nc.vector.tensor_copy(out=dst[:, :VECTOR_GROUPS_W2, :, :], in_=src[:, :VECTOR_GROUPS_W2, :, :])
+                nc.scalar.copy(out=dst[:, VECTOR_GROUPS_W2:, :, :], in_=src[:, VECTOR_GROUPS_W2:, :, :])
+            else:
+                nc.scalar.copy(out=dst, in_=src)
+            start_next_load()
+            v_codes = second_codes.tile([P, N], U32, name="v_codes", tag="v_codes", align_bytes=64)
+            v_scales = second_codes.tile([P, N], U8, name="v_scales", tag="v_scales", align_bytes=64)
+            nc.vector.quantize_mx(out=v_codes[:].bitcast(FP8X4), scales=v_scales[:], in_=v_grouped[:])
+            return v_codes, v_scales
+
+        open_pair = {}
+
+        def place_in_pair(e):
+            return (e % 2) * C if e < E - LATE else 0
+
+        def second_layer(e, h_codes, h_scales, v_codes, v_scales):
+            last = e == E - 1
+            if last:
+                y_lo = psum.tile([P, C], F32, name="y_ps", tag="y_ps")
+                y_hi = psum.tile([P, C], F32, name="y_ps", tag="y_ps")
+                y_blocks = (y_lo[:], y_hi[:])
+            else:
+                y_ps = psum.tile([P, BLOCKS, C], F32, name="y_ps", tag="y_ps")
+                y_blocks = (y_ps[:, 0, :], y_ps[:, 1, :])
+            for b in range(BLOCKS):
+                cols = slice(b * P, (b + 1) * P)
+                nc.tensor.matmul_mx(
+                    out=y_blocks[b],
+                    lhsT=v_codes[:, cols].bitcast(FP8X4),
+                    lhsT_scale=v_scales[:, cols],
+                    rhs=h_codes[:].bitcast(FP8X4),
+                    rhs_scale=h_scales[:],
+                    start=True,
+                    stop=True,
+                )
+            place = place_in_pair(e)
+            if place == 0:
+                y_new = small.tile([P, BLOCKS, 2 * C], F32, name="y_sb", tag="y_sb")
+                open_pair["y"] = y_new
+            y_sb = open_pair["y"]
+            if last:
+                for b in range(BLOCKS):
+                    nc.scalar.copy(out=y_sb[:, b, 0:C], in_=y_blocks[b])
+            else:
+                nc.scalar.copy(out=y_sb[:, :, place : place + C], in_=y_ps[:])
+            return y_sb
+
+        def way_back(e, y_sb):
+            place = place_in_pair(e)
+            first = e * C - place
+            count = place + C
+            if e >= E - LATE or place > 0:
+                for b in range(BLOCKS):
+                    nc.vector.tensor_tensor(
+                        out=window[b][:].indirect(offs_t[:, first // 16 : (first + count) // 16]),
+                        in0=y_sb[:, b, 0:count],
+                        in1=gate_sb[b][:, first : first + count],
+                        op=MULT,
+                    )
+
+        held = []
+        for e in range(E):
+            hidden = first_layer(e)
+            if e < E - LATE:
+                second = second_weights(e)
+                way_back(e, second_layer(e, hidden[0], hidden[1], second[0], second[1]))
+            else:
+                held.append((e, hidden[0], hidden[1]))
+        late_weights = [second_weights(h[0]) for h in held]
+        late_sums = [second_layer(h[0], h[1], h[2], v[0], v[1]) for h, v in zip(held, late_weights)]
+        for h, y_sb in zip(held, late_sums):
+            way_back(h[0], y_sb)
+
+        for b in range(BLOCKS):
+            nc.sync.dma_start(out[b * P : (b + 1) * P, :], window[b][:])

@@ -24,7 +24,9 @@ LINE = 4
 STAGE_BUFS = 11
 LOADS_BEFORE_GATE = 2 * PASSES + 2 * PASSES + 1
 GATHER = 512
-LATE = 2
+LATE = 1
+PAIRED = 6
+EARLY_SLOTS = PAIRED * C
 SCALAR_TAKES_BOTH = (0, 2, 4)
 VECTOR_GROUPS_W3 = 84
 VECTOR_GROUPS_W2 = 40
@@ -84,16 +86,18 @@ def tile_routed_moe_kernel(tc, xT, w1, w3, w2, gate, offs, out):
                     raw = stage.tile([P, PACK, N], F32, name="raw", tag="raw")
                     nc.sync.dma_start(raw[:], w2_view[key[1], :, :, :])
                 staged[key] = raw
+                if started["count"] == len(loads) - 1:
+                    nc.sync.dma_start(gate_late[:], gate_view[:, :, EARLY_SLOTS:SLOTS])
             started["count"] = started["count"] + 1
 
-        gate_sb = []
         window = []
         for i in range(LOADS_BEFORE_GATE):
             start_next_load()
+        gate_view = gate.rearrange("(b p) s -> p b s", p=P)
+        gate_early = keep.tile([P, BLOCKS, EARLY_SLOTS], F32, name="gate_early")
+        gate_late = keep.tile([P, BLOCKS, SLOTS - EARLY_SLOTS], F32, name="gate_late")
+        nc.sync.dma_start(gate_early[:], gate_view[:, :, 0:EARLY_SLOTS])
         for b in range(BLOCKS):
-            gate_b = keep.tile([P, SLOTS], F32, name="gate%d" % b)
-            nc.sync.dma_start(gate_b[:], gate[b * P : (b + 1) * P, :])
-            gate_sb.append(gate_b)
             window_b = keep.tile([P, T], F32, name="window%d" % b)
             window.append(window_b)
         for i in range(LOADS_BEFORE_GATE, STAGE_BUFS):
@@ -202,7 +206,7 @@ def tile_routed_moe_kernel(tc, xT, w1, w3, w2, gate, offs, out):
         open_pair = {}
 
         def place_in_pair(e):
-            return (e % 2) * C if e < E - LATE else 0
+            return (e % 2) * C if e < PAIRED else 0
 
         def second_layer(e, h_codes, h_scales, v_codes, v_scales):
             last = e == E - 1
@@ -240,24 +244,35 @@ def tile_routed_moe_kernel(tc, xT, w1, w3, w2, gate, offs, out):
             place = place_in_pair(e)
             first = e * C - place
             count = place + C
-            if e >= E - LATE or place > 0:
+            if e >= PAIRED or place > 0:
                 for b in range(BLOCKS):
                     nc.vector.tensor_tensor(
                         out=window[b][:].indirect(offs_t[:, first // 16 : (first + count) // 16]),
                         in0=y_sb[:, b, 0:count],
-                        in1=gate_sb[b][:, first : first + count],
+                        in1=(
+                            gate_early[:, b, first : first + count]
+                            if first < EARLY_SLOTS
+                            else gate_late[:, b, first - EARLY_SLOTS : first - EARLY_SLOTS + count]
+                        ),
                         op=MULT,
                     )
 
         held = []
+        unscattered = []
         for e in range(E):
             hidden = first_layer(e)
             if e < E - LATE:
                 second = second_weights(e)
-                way_back(e, second_layer(e, hidden[0], hidden[1], second[0], second[1]))
+                y_done = second_layer(e, hidden[0], hidden[1], second[0], second[1])
+                if e < PAIRED:
+                    way_back(e, y_done)
+                else:
+                    unscattered.append((e, y_done))
             else:
                 held.append((e, hidden[0], hidden[1]))
         late_weights = [second_weights(h[0]) for h in held]
+        for u in unscattered:
+            way_back(u[0], u[1])
         late_sums = [second_layer(h[0], h[1], h[2], v[0], v[1]) for h, v in zip(held, late_weights)]
         for h, y_sb in zip(held, late_sums):
             way_back(h[0], y_sb)

@@ -192,11 +192,7 @@ def tile_routed_moe_kernel(tc, xT, w1, w3, w2, gate, offs, out):
             v_grouped = grouped_pool.tile([P, PACK * N], BF16, name="v_grouped", tag="v_grouped", align_bytes=64)
             dst = v_grouped[:].rearrange("p (c i j) -> p c j i", i=LINE, j=PACK)
             src = raw[:].rearrange("p j (c i) -> p c j i", i=LINE)
-            if e == E - 1:
-                nc.vector.tensor_copy(out=dst[:, :VECTOR_GROUPS_W2, :, :], in_=src[:, :VECTOR_GROUPS_W2, :, :])
-                nc.scalar.copy(out=dst[:, VECTOR_GROUPS_W2:, :, :], in_=src[:, VECTOR_GROUPS_W2:, :, :])
-            else:
-                nc.scalar.copy(out=dst, in_=src)
+            nc.scalar.copy(out=dst, in_=src)
             start_next_load()
             v_codes = second_codes.tile([P, N], U32, name="v_codes", tag="v_codes", align_bytes=64)
             v_scales = second_codes.tile([P, N], U8, name="v_scales", tag="v_scales", align_bytes=64)

@@ -25,8 +25,9 @@ STAGE_BUFS = 11
 LOADS_BEFORE_GATE = 2 * PASSES + 2 * PASSES + 1
 GATHER = 512
 LATE = 1
-PAIRED = 6
-EARLY_SLOTS = PAIRED * C
+PAIRED = 4
+WAIT_FROM = 6
+EARLY_SLOTS = WAIT_FROM * C
 SCALAR_TAKES_BOTH = (0, 2, 4)
 VECTOR_GROUPS_W3 = 84
 VECTOR_GROUPS_W2 = 40
@@ -260,7 +261,7 @@ def tile_routed_moe_kernel(tc, xT, w1, w3, w2, gate, offs, out):
             if e < E - LATE:
                 second = second_weights(e)
                 y_done = second_layer(e, hidden[0], hidden[1], second[0], second[1])
-                if e < PAIRED:
+                if e < WAIT_FROM:
                     way_back(e, y_done)
                 else:
                     unscattered.append((e, y_done))

@@ -42,7 +42,9 @@ def tile_routed_moe_kernel(tc, xT, w1, w3, w2, gate, offs, out):
         first_codes = ctx.enter_context(tc.tile_pool(name="first_codes", bufs=5))
         second_codes = ctx.enter_context(tc.tile_pool(name="second_codes", bufs=3))
         small = ctx.enter_context(tc.tile_pool(name="small", bufs=3))
+        turns = ctx.enter_context(tc.tile_pool(name="turns", bufs=1))
         psum = ctx.enter_context(tc.psum_pool(name="psum", bufs=2))
+        y_psum = ctx.enter_context(tc.psum_pool(name="y_psum", bufs=4))
 
         offs_t = keep.tile([P, SLOTS // 16], U16, name="offs_t")
         nc.sync.dma_start(offs_t[:], offs)
@@ -112,10 +114,12 @@ def tile_routed_moe_kernel(tc, xT, w1, w3, w2, gate, offs, out):
             for u in range(2):
                 raw = staged[("x", g, u)]
                 x_pairs = keep.tile([P, 2 * T], BF16, name="x_pairs%d%d" % (g, u))
-                nc.scalar.copy(
-                    out=x_pairs[:].rearrange("p (c i r) -> p c r i", i=LINE, r=2),
-                    in_=raw[:].rearrange("p r (c i) -> p c r i", i=LINE),
-                )
+                x_dst = x_pairs[:].rearrange("p (c i r) -> p c r i", i=LINE, r=2)
+                x_src = raw[:].rearrange("p r (c i) -> p c r i", i=LINE)
+                if g == 0 and u == 0:
+                    nc.vector.tensor_copy(out=x_dst, in_=x_src)
+                else:
+                    nc.scalar.copy(out=x_dst, in_=x_src)
                 start_next_load()
                 for s0 in range(0, SLOTS, GATHER):
                     nc.vector.tensor_copy(
@@ -177,15 +181,28 @@ def tile_routed_moe_kernel(tc, xT, w1, w3, w2, gate, offs, out):
                             start=(g == 0),
                             stop=(g == PASSES - 1),
                         )
-            silu_a = small.tile([P, C, PACK], F32, name="silu_a", tag="silu_a")
+            if e == E - 1:
+                silu_a = turns.tile([P, C, PACK], F32, name="silu_last", tag="turn")
+            else:
+                silu_a = small.tile([P, C, PACK], F32, name="silu_a", tag="silu_a")
             nc.scalar.activation(out=silu_a[:], in_=a_ps[:].rearrange("p t c -> p c t"), func=SILU)
             h_grouped = small.tile([P, C, PACK], BF16, name="h_grouped", tag="h_grouped", align_bytes=64)
-            nc.vector.tensor_tensor(out=h_grouped[:], in0=b_ps[:].rearrange("p t c -> p c t"), in1=silu_a[:], op=MULT)
             h_codes = small.tile([P, C], U32, name="h_codes", tag="h_codes", align_bytes=64)
             h_scales = small.tile([P, C], U8, name="h_scales", tag="h_scales", align_bytes=64)
-            nc.vector.quantize_mx(
-                out=h_codes[:].bitcast(FP8X4), scales=h_scales[:], in_=h_grouped[:].rearrange("p c t -> p (c t)")
-            )
+            half = C // 2 if e == E - 1 else C
+            for c0 in range(0, C, half):
+                nc.vector.tensor_tensor(
+                    out=h_grouped[:, c0 : c0 + half, :],
+                    in0=b_ps[:, :, c0 : c0 + half].rearrange("p t c -> p c t"),
+                    in1=silu_a[:, c0 : c0 + half, :],
+                    op=MULT,
+                )
+            for c0 in range(0, C, half):
+                nc.vector.quantize_mx(
+                    out=h_codes[:, c0 : c0 + half].bitcast(FP8X4),
+                    scales=h_scales[:, c0 : c0 + half],
+                    in_=h_grouped[:, c0 : c0 + half, :].rearrange("p c t -> p (c t)"),
+                )
             return h_codes, h_scales
 
         def second_weights(e):
@@ -208,11 +225,11 @@ def tile_routed_moe_kernel(tc, xT, w1, w3, w2, gate, offs, out):
         def second_layer(e, h_codes, h_scales, v_codes, v_scales):
             last = e == E - 1
             if last:
-                y_lo = psum.tile([P, C], F32, name="y_ps", tag="y_ps")
-                y_hi = psum.tile([P, C], F32, name="y_ps", tag="y_ps")
+                y_lo = y_psum.tile([P, C], F32, name="y_ps", tag="y_ps")
+                y_hi = y_psum.tile([P, C], F32, name="y_ps", tag="y_ps")
                 y_blocks = (y_lo[:], y_hi[:])
             else:
-                y_ps = psum.tile([P, BLOCKS, C], F32, name="y_ps", tag="y_ps")
+                y_ps = y_psum.tile([P, BLOCKS, C], F32, name="y_ps", tag="y_ps")
                 y_blocks = (y_ps[:, 0, :], y_ps[:, 1, :])
             for b in range(BLOCKS):
                 cols = slice(b * P, (b + 1) * P)
@@ -233,6 +250,9 @@ def tile_routed_moe_kernel(tc, xT, w1, w3, w2, gate, offs, out):
             if last:
                 for b in range(BLOCKS):
                     nc.scalar.copy(out=y_sb[:, b, 0:C], in_=y_blocks[b])
+            elif e >= WAIT_FROM:
+                nc.scalar.copy(out=y_sb[:, 0, 0:C], in_=y_ps[:, 0, :])
+                open_pair["y_ps"] = y_ps
             else:
                 nc.scalar.copy(out=y_sb[:, :, place : place + C], in_=y_ps[:])
             return y_sb
@@ -269,7 +289,16 @@ def tile_routed_moe_kernel(tc, xT, w1, w3, w2, gate, offs, out):
                 held.append((e, hidden[0], hidden[1]))
         late_weights = [second_weights(h[0]) for h in held]
         for u in unscattered:
-            way_back(u[0], u[1])
+            first = u[0] * C
+            y_turn = turns.tile([P, C], F32, name="y_turn", tag="turn")
+            nc.scalar.copy(out=y_turn[:], in_=open_pair["y_ps"][:, 1, :])
+            for b, y_b in ((0, u[1][:, 0, 0:C]), (1, y_turn[:])):
+                nc.vector.tensor_tensor(
+                    out=window[b][:].indirect(offs_t[:, first // 16 : (first + C) // 16]),
+                    in0=y_b,
+                    in1=gate_late[:, b, first - EARLY_SLOTS : first - EARLY_SLOTS + C],
+                    op=MULT,
+                )
         late_sums = [second_layer(h[0], h[1], h[2], v[0], v[1]) for h, v in zip(held, late_weights)]
         for h, y_sb in zip(held, late_sums):
             way_back(h[0], y_sb)

@@ -144,7 +144,23 @@ def tile_routed_moe_kernel(tc, xT, w1, w3, w2, gate, offs, out):
                     raw = staged[("first", e, m, g)]
                     dst = w_grouped[:, g * PACK * H : (g + 1) * PACK * H].rearrange("p (t q j) -> p q j t", t=PACK, q=P, j=PACK)
                     src = raw[:].rearrange("p j (q t) -> p q j t", t=PACK)
-                    if last and m == 1:
+                    if last and m == 1 and g == PASSES - 1:
+                        dst_h = w_grouped[:, g * PACK * H : (g + 1) * PACK * H].rearrange(
+                            "p (a b q j) -> p a q j b", a=2, b=2, q=P, j=PACK
+                        )
+                        src_h = raw[:].rearrange("p j (q a b) -> p a q j b", a=2, b=2)
+                        for a in range(2):
+                            n_v = P if a == 0 else P // 2
+                            nc.vector.tensor_copy(out=dst_h[:, a, :n_v, :, :], in_=src_h[:, a, :n_v, :, :])
+                            if n_v < P:
+                                nc.scalar.copy(out=dst_h[:, a, n_v:, :, :], in_=src_h[:, a, n_v:, :, :])
+                            c0 = g * H + a * H // 2
+                            nc.vector.quantize_mx(
+                                out=codes[:, c0 : c0 + H // 2].bitcast(FP8X4),
+                                scales=scales[:, c0 : c0 + H // 2],
+                                in_=w_grouped[:, PACK * c0 : PACK * (c0 + H // 2)],
+                            )
+                    elif last and m == 1:
                         nc.vector.tensor_copy(out=dst[:, :VECTOR_GROUPS_W3, :, :], in_=src[:, :VECTOR_GROUPS_W3, :, :])
                         nc.scalar.copy(out=dst[:, VECTOR_GROUPS_W3:, :, :], in_=src[:, VECTOR_GROUPS_W3:, :, :])
                     elif g == 0 or (m == 0 and e in SCALAR_TAKES_BOTH):
@@ -152,16 +168,13 @@ def tile_routed_moe_kernel(tc, xT, w1, w3, w2, gate, offs, out):
                     else:
                         nc.vector.tensor_copy(out=dst, in_=src)
                     start_next_load()
-                    if last:
-                        calls = 2 if m == 1 and g == PASSES - 1 else 1
-                        width = H // calls
-                        for c0 in range(g * H, (g + 1) * H, width):
-                            nc.vector.quantize_mx(
-                                out=codes[:, c0 : c0 + width].bitcast(FP8X4),
-                                scales=scales[:, c0 : c0 + width],
-                                in_=w_grouped[:, PACK * c0 : PACK * (c0 + width)],
-                            )
-                if not last:
+                    if last and m == 1 and g < PASSES - 1:
+                        nc.vector.quantize_mx(
+                            out=codes[:, g * H : (g + 1) * H].bitcast(FP8X4),
+                            scales=scales[:, g * H : (g + 1) * H],
+                            in_=w_grouped[:, g * PACK * H : (g + 1) * PACK * H],
+                        )
+                if not (last and m == 1):
                     nc.vector.quantize_mx(out=codes[:].bitcast(FP8X4), scales=scales[:], in_=w_grouped[:])
                 quantised.append((codes, scales))
 

@@ -25,7 +25,6 @@ STAGE_BUFS = 11
 LOADS_BEFORE_GATE = 2 * PASSES + 2 * PASSES + 1
 GATHER = 512
 LATE = 1
-PAIRED = 4
 WAIT_FROM = 6
 EARLY_SLOTS = WAIT_FROM * C
 SCALAR_TAKES_BOTH = (0, 2, 4)
@@ -154,12 +153,14 @@ def tile_routed_moe_kernel(tc, xT, w1, w3, w2, gate, offs, out):
                             nc.vector.tensor_copy(out=dst_h[:, a, :n_v, :, :], in_=src_h[:, a, :n_v, :, :])
                             if n_v < P:
                                 nc.scalar.copy(out=dst_h[:, a, n_v:, :, :], in_=src_h[:, a, n_v:, :, :])
-                            c0 = g * H + a * H // 2
-                            nc.vector.quantize_mx(
-                                out=codes[:, c0 : c0 + H // 2].bitcast(FP8X4),
-                                scales=scales[:, c0 : c0 + H // 2],
-                                in_=w_grouped[:, PACK * c0 : PACK * (c0 + H // 2)],
-                            )
+                            calls = 1 if a == 0 else 2
+                            cut = H // 2 // calls
+                            for c0 in range(g * H + a * H // 2, g * H + (a + 1) * H // 2, cut):
+                                nc.vector.quantize_mx(
+                                    out=codes[:, c0 : c0 + cut].bitcast(FP8X4),
+                                    scales=scales[:, c0 : c0 + cut],
+                                    in_=w_grouped[:, PACK * c0 : PACK * (c0 + cut)],
+                                )
                     elif last and m == 1:
                         nc.vector.tensor_copy(out=dst[:, :VECTOR_GROUPS_W3, :, :], in_=src[:, :VECTOR_GROUPS_W3, :, :])
                         nc.scalar.copy(out=dst[:, VECTOR_GROUPS_W3:, :, :], in_=src[:, VECTOR_GROUPS_W3:, :, :])
@@ -202,7 +203,7 @@ def tile_routed_moe_kernel(tc, xT, w1, w3, w2, gate, offs, out):
             h_grouped = small.tile([P, C, PACK], BF16, name="h_grouped", tag="h_grouped", align_bytes=64)
             h_codes = small.tile([P, C], U32, name="h_codes", tag="h_codes", align_bytes=64)
             h_scales = small.tile([P, C], U8, name="h_scales", tag="h_scales", align_bytes=64)
-            half = C // 2 if e == E - 1 else C
+            half = C // 2
             for c0 in range(0, C, half):
                 nc.vector.tensor_tensor(
                     out=h_grouped[:, c0 : c0 + half, :],
@@ -230,20 +231,7 @@ def tile_routed_moe_kernel(tc, xT, w1, w3, w2, gate, offs, out):
             nc.vector.quantize_mx(out=v_codes[:].bitcast(FP8X4), scales=v_scales[:], in_=v_grouped[:])
             return v_codes, v_scales
 
-        open_pair = {}
-
-        def place_in_pair(e):
-            return (e % 2) * C if e < PAIRED else 0
-
-        def second_layer(e, h_codes, h_scales, v_codes, v_scales):
-            last = e == E - 1
-            if last:
-                y_lo = y_psum.tile([P, C], F32, name="y_ps", tag="y_ps")
-                y_hi = y_psum.tile([P, C], F32, name="y_ps", tag="y_ps")
-                y_blocks = (y_lo[:], y_hi[:])
-            else:
-                y_ps = y_psum.tile([P, BLOCKS, C], F32, name="y_ps", tag="y_ps")
-                y_blocks = (y_ps[:, 0, :], y_ps[:, 1, :])
+        def products(y_blocks, h_codes, h_scales, v_codes, v_scales):
             for b in range(BLOCKS):
                 cols = slice(b * P, (b + 1) * P)
                 nc.tensor.matmul_mx(
@@ -255,66 +243,49 @@ def tile_routed_moe_kernel(tc, xT, w1, w3, w2, gate, offs, out):
                     start=True,
                     stop=True,
                 )
-            place = place_in_pair(e)
-            if place == 0:
-                y_new = small.tile([P, BLOCKS, 2 * C], F32, name="y_sb", tag="y_sb")
-                open_pair["y"] = y_new
-            y_sb = open_pair["y"]
-            if last:
-                for b in range(BLOCKS):
-                    nc.scalar.copy(out=y_sb[:, b, 0:C], in_=y_blocks[b])
-            elif e >= WAIT_FROM:
-                nc.scalar.copy(out=y_sb[:, 0, 0:C], in_=y_ps[:, 0, :])
-                open_pair["y_ps"] = y_ps
+
+        def scatter(b, e, count, y):
+            first = e * C
+            if e < WAIT_FROM:
+                gate_weights = gate_early[:, b, first : first + count]
             else:
-                nc.scalar.copy(out=y_sb[:, :, place : place + C], in_=y_ps[:])
-            return y_sb
+                gate_weights = gate_late[:, b, first - EARLY_SLOTS : first - EARLY_SLOTS + count]
+            nc.vector.tensor_tensor(
+                out=window[b][:].indirect(offs_t[:, first // 16 : (first + count) // 16]), in0=y, in1=gate_weights, op=MULT
+            )
 
-        def way_back(e, y_sb):
-            place = place_in_pair(e)
-            first = e * C - place
-            count = place + C
-            if e >= PAIRED or place > 0:
-                for b in range(BLOCKS):
-                    nc.vector.tensor_tensor(
-                        out=window[b][:].indirect(offs_t[:, first // 16 : (first + count) // 16]),
-                        in0=y_sb[:, b, 0:count],
-                        in1=(
-                            gate_early[:, b, first : first + count]
-                            if first < EARLY_SLOTS
-                            else gate_late[:, b, first - EARLY_SLOTS : first - EARLY_SLOTS + count]
-                        ),
-                        op=MULT,
-                    )
-
-        held = []
-        unscattered = []
+        hidden = []
+        late_y = {}
         for e in range(E):
-            hidden = first_layer(e)
+            hidden.append(first_layer(e))
             if e < E - LATE:
                 second = second_weights(e)
-                y_done = second_layer(e, hidden[0], hidden[1], second[0], second[1])
+                y_ps = y_psum.tile([P, BLOCKS, C], F32, name="y_ps", tag="y_ps")
+                products((y_ps[:, 0, :], y_ps[:, 1, :]), hidden[e][0], hidden[e][1], second[0], second[1])
+                y_sb = small.tile([P, BLOCKS, C], F32, name="y_sb", tag="y_sb")
                 if e < WAIT_FROM:
-                    way_back(e, y_done)
+                    nc.scalar.copy(out=y_sb[:], in_=y_ps[:])
+                    for b in range(BLOCKS):
+                        scatter(b, e, C, y_sb[:, b, :])
                 else:
-                    unscattered.append((e, y_done))
-            else:
-                held.append((e, hidden[0], hidden[1]))
-        late_weights = [second_weights(h[0]) for h in held]
-        for u in unscattered:
-            first = u[0] * C
-            y_turn = turns.tile([P, C], F32, name="y_turn", tag="turn")
-            nc.scalar.copy(out=y_turn[:], in_=open_pair["y_ps"][:, 1, :])
-            for b, y_b in ((0, u[1][:, 0, 0:C]), (1, y_turn[:])):
-                nc.vector.tensor_tensor(
-                    out=window[b][:].indirect(offs_t[:, first // 16 : (first + C) // 16]),
-                    in0=y_b,
-                    in1=gate_late[:, b, first - EARLY_SLOTS : first - EARLY_SLOTS + C],
-                    op=MULT,
-                )
-        late_sums = [second_layer(h[0], h[1], h[2], v[0], v[1]) for h, v in zip(held, late_weights)]
-        for h, y_sb in zip(held, late_sums):
-            way_back(h[0], y_sb)
+                    nc.scalar.copy(out=y_sb[:, 0, :], in_=y_ps[:, 0, :])
+                    late_y[e] = (y_ps, y_sb)
+        second = second_weights(E - 1)
+
+        y_ps, y_sb = late_y[E - 2]
+        y_turn = turns.tile([P, C], F32, name="y_turn", tag="turn")
+        nc.scalar.copy(out=y_turn[:], in_=y_ps[:, 1, :])
+        scatter(0, E - 2, C, y_sb[:, 0, :])
+        scatter(1, E - 2, C, y_turn[:])
+
+        y_lo = y_psum.tile([P, C], F32, name="y_lo", tag="y_ps")
+        y_hi = y_psum.tile([P, C], F32, name="y_hi", tag="y_ps")
+        products((y_lo[:], y_hi[:]), hidden[E - 1][0], hidden[E - 1][1], second[0], second[1])
+        y_sb = small.tile([P, BLOCKS, C], F32, name="y_sb", tag="y_sb")
+        nc.scalar.copy(out=y_sb[:, 0, :], in_=y_lo[:])
+        nc.scalar.copy(out=y_sb[:, 1, :], in_=y_hi[:])
+        for b in range(BLOCKS):
+            scatter(b, E - 1, C, y_sb[:, b, :])
 
         for b in range(BLOCKS):
             nc.sync.dma_start(out[b * P : (b + 1) * P, :], window[b][:])

@@ -27,7 +27,7 @@ GATHER = 512
 LATE = 1
 WAIT_FROM = 6
 EARLY_SLOTS = WAIT_FROM * C
-SCALAR_TAKES_BOTH = (0, 2, 4)
+SCALAR_TAKES_BOTH = (0,)
 VECTOR_GROUPS_W3 = 84
 VECTOR_GROUPS_W2 = 40
 
@@ -161,7 +161,7 @@ def tile_routed_moe_kernel(tc, xT, w1, w3, w2, gate, offs, out):
                                     scales=scales[:, c0 : c0 + cut],
                                     in_=w_grouped[:, PACK * c0 : PACK * (c0 + cut)],
                                 )
-                    elif last and m == 1:
+                    elif (last and m == 1) or (m == 0 and g == 1 and 0 < e < E - 1):
                         nc.vector.tensor_copy(out=dst[:, :VECTOR_GROUPS_W3, :, :], in_=src[:, :VECTOR_GROUPS_W3, :, :])
                         nc.scalar.copy(out=dst[:, VECTOR_GROUPS_W3:, :, :], in_=src[:, VECTOR_GROUPS_W3:, :, :])
                     elif g == 0 or (m == 0 and e in SCALAR_TAKES_BOTH):

from contextlib import ExitStack

import concourse.mybir as mybir

K, T, E, C, H, N = 1024, 1024, 8, 128, 512, 256
FLOPS = 2 * E * C * (2 * K * H + H * N)

F32 = mybir.dt.float32
BF16 = mybir.dt.bfloat16
U32 = mybir.dt.uint32
U16 = mybir.dt.uint16
U8 = mybir.dt.uint8
FP8X4 = mybir.dt.float8_e4m3fn_x4
MULT = mybir.AluOpType.mult
SILU = mybir.ActivationFunctionType.Silu

P = 128
PACK = 4
PASSES = K // (P * PACK)
SLOTS = E * C
BLOCKS = N // P
LINE = 4

STAGE_BUFS = 11
LOADS_BEFORE_GATE = 2 * PASSES + 2 * PASSES + 1
GATHER = 512
LATE = 1
WAIT_FROM = 6
EARLY_SLOTS = WAIT_FROM * C
SCALAR_TAKES_BOTH = (0,)
VECTOR_GROUPS_W3 = 84
VECTOR_GROUPS_W2 = 40


def tile_routed_moe_kernel(tc, xT, w1, w3, w2, gate, offs, out):
    nc = tc.nc
    with ExitStack() as ctx:
        keep = ctx.enter_context(tc.tile_pool(name="keep", bufs=1))
        stage = ctx.enter_context(tc.tile_pool(name="stage", bufs=STAGE_BUFS))
        grouped_pool = ctx.enter_context(tc.tile_pool(name="grouped", bufs=3))
        first_codes = ctx.enter_context(tc.tile_pool(name="first_codes", bufs=5))
        second_codes = ctx.enter_context(tc.tile_pool(name="second_codes", bufs=3))
        small = ctx.enter_context(tc.tile_pool(name="small", bufs=3))
        turns = ctx.enter_context(tc.tile_pool(name="turns", bufs=1))
        psum = ctx.enter_context(tc.psum_pool(name="psum", bufs=2))
        y_psum = ctx.enter_context(tc.psum_pool(name="y_psum", bufs=4))

        offs_t = keep.tile([P, SLOTS // 16], U16, name="offs_t")
        nc.sync.dma_start(offs_t[:], offs)

        table_in = keep.tile([P, 1], F32, name="table_in")
        table_out = keep.tile([P, 1], F32, name="table_out")
        nc.vector.memset(table_in[:], 0.0)
        nc.scalar.activation(out=table_out[:], in_=table_in[:], func=SILU)

        x_view = xT.rearrange("(g p u r) n -> g u p r n", g=PASSES, p=P, u=2, r=2)
        first_views = (
            w1.rearrange("e (g p j) c -> e g p j c", g=PASSES, p=P, j=PACK),
            w3.rearrange("e (g p j) c -> e g p j c", g=PASSES, p=P, j=PACK),
        )
        w2_view = w2.rearrange("e (p j) n -> e p j n", p=P, j=PACK)

        loads = []
        for g in range(PASSES):
            for u in range(2):
                loads.append(("x", g, u))
        for e in range(E):
            for m in range(2):
                for g in range(PASSES):
                    loads.append(("first", e, m, g))
            if e < E - LATE:
                loads.append(("second", e))
        for e in range(E - LATE, E):
            loads.append(("second", e))
        staged = {}
        started = {"count": 0}

        def start_next_load():
            if started["count"] < len(loads):
                key = loads[started["count"]]
                if key[0] == "x":
                    raw = stage.tile([P, 2, T], F32, name="raw", tag="raw")
                    nc.sync.dma_start(raw[:], x_view[key[1], key[2], :, :, :])
                elif key[0] == "first":
                    raw = stage.tile([P, PACK, H], F32, name="raw", tag="raw")
                    nc.sync.dma_start(raw[:], first_views[key[2]][key[1], key[3], :, :, :])
                else:
                    raw = stage.tile([P, PACK, N], F32, name="raw", tag="raw")
                    nc.sync.dma_start(raw[:], w2_view[key[1], :, :, :])
                staged[key] = raw
                if started["count"] == len(loads) - 1:
                    nc.sync.dma_start(gate_late[:], gate_view[:, :, EARLY_SLOTS:SLOTS])
            started["count"] = started["count"] + 1

        window = []
        for i in range(LOADS_BEFORE_GATE):
            start_next_load()
        gate_view = gate.rearrange("(b p) s -> p b s", p=P)
        gate_early = keep.tile([P, BLOCKS, EARLY_SLOTS], F32, name="gate_early")
        gate_late = keep.tile([P, BLOCKS, SLOTS - EARLY_SLOTS], F32, name="gate_late")
        nc.sync.dma_start(gate_early[:], gate_view[:, :, 0:EARLY_SLOTS])
        for b in range(BLOCKS):
            window_b = keep.tile([P, T], F32, name="window%d" % b)
            window.append(window_b)
        for i in range(LOADS_BEFORE_GATE, STAGE_BUFS):
            start_next_load()

        x_codes = []
        x_scales = []
        for g in range(PASSES):
            x_grouped = keep.tile([P, PACK * SLOTS], BF16, name="x_grouped%d" % g, align_bytes=64)
            x_words = x_grouped[:].bitcast(U32).rearrange("p (s u) -> p s u", u=2)
            for u in range(2):
                raw = staged[("x", g, u)]
                x_pairs = keep.tile([P, 2 * T], BF16, name="x_pairs%d%d" % (g, u))
                x_dst = x_pairs[:].rearrange("p (c i r) -> p c r i", i=LINE, r=2)
                x_src = raw[:].rearrange("p r (c i) -> p c r i", i=LINE)
                if g == 0 and u == 0:
                    nc.vector.tensor_copy(out=x_dst, in_=x_src)
                else:
                    nc.scalar.copy(out=x_dst, in_=x_src)
                start_next_load()
                for s0 in range(0, SLOTS, GATHER):
                    nc.vector.tensor_copy(
                        out=x_words[:, s0 : s0 + GATHER, u],
                        in_=x_pairs[:].bitcast(U32).indirect(offs_t[:, s0 // 16 : (s0 + GATHER) // 16]),
                    )
            x_codes_g = keep.tile([P, SLOTS], U32, name="x_codes%d" % g, align_bytes=64)
            x_scales_g = keep.tile([P, SLOTS], U8, name="x_scales%d" % g, align_bytes=64)
            nc.vector.quantize_mx(out=x_codes_g[:].bitcast(FP8X4), scales=x_scales_g[:], in_=x_grouped[:])
            x_codes.append(x_codes_g)
            x_scales.append(x_scales_g)

        def first_layer(e):
            slots = slice(e * C, (e + 1) * C)
            last = e == E - 1
            quantised = []
            for m in range(2):
                w_grouped = grouped_pool.tile([P, PASSES * PACK * H], BF16, name="w_grouped", tag="w_grouped", align_bytes=64)
                codes = first_codes.tile([P, PASSES * H], U32, name="w_codes", tag="w_codes", align_bytes=64)
                scales = first_codes.tile([P, PASSES * H], U8, name="w_scales", tag="w_scales", align_bytes=64)
                for g in range(PASSES):
                    raw = staged[("first", e, m, g)]
                    dst = w_grouped[:, g * PACK * H : (g + 1) * PACK * H].rearrange("p (t q j) -> p q j t", t=PACK, q=P, j=PACK)
                    src = raw[:].rearrange("p j (q t) -> p q j t", t=PACK)
                    if last and m == 1 and g == PASSES - 1:
                        dst_h = w_grouped[:, g * PACK * H : (g + 1) * PACK * H].rearrange(
                            "p (a b q j) -> p a q j b", a=2, b=2, q=P, j=PACK
                        )
                        src_h = raw[:].rearrange("p j (q a b) -> p a q j b", a=2, b=2)
                        for a in range(2):
                            n_v = P if a == 0 else P // 2
                            nc.vector.tensor_copy(out=dst_h[:, a, :n_v, :, :], in_=src_h[:, a, :n_v, :, :])
                            if n_v < P:
                                nc.scalar.copy(out=dst_h[:, a, n_v:, :, :], in_=src_h[:, a, n_v:, :, :])
                            calls = 1 if a == 0 else 2
                            cut = H // 2 // calls
                            for c0 in range(g * H + a * H // 2, g * H + (a + 1) * H // 2, cut):
                                nc.vector.quantize_mx(
                                    out=codes[:, c0 : c0 + cut].bitcast(FP8X4),
                                    scales=scales[:, c0 : c0 + cut],
                                    in_=w_grouped[:, PACK * c0 : PACK * (c0 + cut)],
                                )
                    elif (last and m == 1) or (m == 0 and g == 1 and 0 < e < E - 1):
                        nc.vector.tensor_copy(out=dst[:, :VECTOR_GROUPS_W3, :, :], in_=src[:, :VECTOR_GROUPS_W3, :, :])
                        nc.scalar.copy(out=dst[:, VECTOR_GROUPS_W3:, :, :], in_=src[:, VECTOR_GROUPS_W3:, :, :])
                    elif g == 0 or (m == 0 and e in SCALAR_TAKES_BOTH):
                        nc.scalar.copy(out=dst, in_=src)
                    else:
                        nc.vector.tensor_copy(out=dst, in_=src)
                    start_next_load()
                    if last and m == 1 and g < PASSES - 1:
                        nc.vector.quantize_mx(
                            out=codes[:, g * H : (g + 1) * H].bitcast(FP8X4),
                            scales=scales[:, g * H : (g + 1) * H],
                            in_=w_grouped[:, g * PACK * H : (g + 1) * PACK * H],
                        )
                if not (last and m == 1):
                    nc.vector.quantize_mx(out=codes[:].bitcast(FP8X4), scales=scales[:], in_=w_grouped[:])
                quantised.append((codes, scales))

            a_ps = psum.tile([P, PACK, C], F32, name="a_ps", tag="a_ps")
            b_ps = psum.tile([P, PACK, C], F32, name="b_ps", tag="b_ps")
            for m, acc in ((0, a_ps), (1, b_ps)):
                codes, scales = quantised[m]
                for t in range(PACK):
                    for g in range(PASSES):
                        cols = slice(g * H + t * P, g * H + (t + 1) * P)
                        nc.tensor.matmul_mx(
                            out=acc[:, t, :],
                            lhsT=codes[:, cols].bitcast(FP8X4),
                            lhsT_scale=scales[:, cols],
                            rhs=x_codes[g][:, slots].bitcast(FP8X4),
                            rhs_scale=x_scales[g][:, slots],
                            start=(g == 0),
                            stop=(g == PASSES - 1),
                        )
            if e == E - 1:
                silu_a = turns.tile([P, C, PACK], F32, name="silu_last", tag="turn")
            else:
                silu_a = small.tile([P, C, PACK], F32, name="silu_a", tag="silu_a")
            nc.scalar.activation(out=silu_a[:], in_=a_ps[:].rearrange("p t c -> p c t"), func=SILU)
            h_grouped = small.tile([P, C, PACK], BF16, name="h_grouped", tag="h_grouped", align_bytes=64)
            h_codes = small.tile([P, C], U32, name="h_codes", tag="h_codes", align_bytes=64)
            h_scales = small.tile([P, C], U8, name="h_scales", tag="h_scales", align_bytes=64)
            half = C // 2
            for c0 in range(0, C, half):
                nc.vector.tensor_tensor(
                    out=h_grouped[:, c0 : c0 + half, :],
                    in0=b_ps[:, :, c0 : c0 + half].rearrange("p t c -> p c t"),
                    in1=silu_a[:, c0 : c0 + half, :],
                    op=MULT,
                )
            for c0 in range(0, C, half):
                nc.vector.quantize_mx(
                    out=h_codes[:, c0 : c0 + half].bitcast(FP8X4),
                    scales=h_scales[:, c0 : c0 + half],
                    in_=h_grouped[:, c0 : c0 + half, :].rearrange("p c t -> p (c t)"),
                )
            return h_codes, h_scales

        def second_weights(e):
            raw = staged[("second", e)]
            v_grouped = grouped_pool.tile([P, PACK * N], BF16, name="v_grouped", tag="v_grouped", align_bytes=64)
            dst = v_grouped[:].rearrange("p (c i j) -> p c j i", i=LINE, j=PACK)
            src = raw[:].rearrange("p j (c i) -> p c j i", i=LINE)
            nc.scalar.copy(out=dst, in_=src)
            start_next_load()
            v_codes = second_codes.tile([P, N], U32, name="v_codes", tag="v_codes", align_bytes=64)
            v_scales = second_codes.tile([P, N], U8, name="v_scales", tag="v_scales", align_bytes=64)
            nc.vector.quantize_mx(out=v_codes[:].bitcast(FP8X4), scales=v_scales[:], in_=v_grouped[:])
            return v_codes, v_scales

        def products(y_blocks, h_codes, h_scales, v_codes, v_scales):
            for b in range(BLOCKS):
                cols = slice(b * P, (b + 1) * P)
                nc.tensor.matmul_mx(
                    out=y_blocks[b],
                    lhsT=v_codes[:, cols].bitcast(FP8X4),
                    lhsT_scale=v_scales[:, cols],
                    rhs=h_codes[:].bitcast(FP8X4),
                    rhs_scale=h_scales[:],
                    start=True,
                    stop=True,
                )

        def scatter(b, e, count, y):
            first = e * C
            if e < WAIT_FROM:
                gate_weights = gate_early[:, b, first : first + count]
            else:
                gate_weights = gate_late[:, b, first - EARLY_SLOTS : first - EARLY_SLOTS + count]
            nc.vector.tensor_tensor(
                out=window[b][:].indirect(offs_t[:, first // 16 : (first + count) // 16]), in0=y, in1=gate_weights, op=MULT
            )

        hidden = []
        late_y = {}
        for e in range(E):
            hidden.append(first_layer(e))
            if e < E - LATE:
                second = second_weights(e)
                y_ps = y_psum.tile([P, BLOCKS, C], F32, name="y_ps", tag="y_ps")
                products((y_ps[:, 0, :], y_ps[:, 1, :]), hidden[e][0], hidden[e][1], second[0], second[1])
                y_sb = small.tile([P, BLOCKS, C], F32, name="y_sb", tag="y_sb")
                if e < WAIT_FROM:
                    nc.scalar.copy(out=y_sb[:], in_=y_ps[:])
                    for b in range(BLOCKS):
                        scatter(b, e, C, y_sb[:, b, :])
                else:
                    nc.scalar.copy(out=y_sb[:, 0, :], in_=y_ps[:, 0, :])
                    late_y[e] = (y_ps, y_sb)
        second = second_weights(E - 1)

        y_ps, y_sb = late_y[E - 2]
        y_turn = turns.tile([P, C], F32, name="y_turn", tag="turn")
        nc.scalar.copy(out=y_turn[:], in_=y_ps[:, 1, :])
        scatter(0, E - 2, C, y_sb[:, 0, :])
        scatter(1, E - 2, C, y_turn[:])

        y_lo = y_psum.tile([P, C], F32, name="y_lo", tag="y_ps")
        y_hi = y_psum.tile([P, C], F32, name="y_hi", tag="y_ps")
        products((y_lo[:], y_hi[:]), hidden[E - 1][0], hidden[E - 1][1], second[0], second[1])
        y_sb = small.tile([P, BLOCKS, C], F32, name="y_sb", tag="y_sb")
        nc.scalar.copy(out=y_sb[:, 0, :], in_=y_lo[:])
        nc.scalar.copy(out=y_sb[:, 1, :], in_=y_hi[:])
        for b in range(BLOCKS):
            scatter(b, E - 1, C, y_sb[:, b, :])

        for b in range(BLOCKS):
            nc.sync.dma_start(out[b * P : (b + 1) * P, :], window[b][:])
